import numpy as np, ml_dtypes
CORES = [2,3,42,43,82,83,122,123]
N = 8
BF = ml_dtypes.bfloat16
def gentries(a):
    return np.ascontiguousarray(a.reshape(8, 16, -1).transpose(0, 2, 1)).reshape(8, -1)
def gtable(e):
    e = np.asarray(e); return np.ascontiguousarray(e.reshape(8, -1, 16).transpose(0, 2, 1)).reshape(128, -1).astype(np.int32)
V, G, L, D, RO = 3072, 64, 768, 4, 3
S = (N - 1) * G; W = V + S
def weave(rng, share, ring=0.03, ends=False, most=V):
    o = rng.permutation(V); b = rng.random(V) < share; b[0] = True
    if ends: o = np.concatenate([np.array([0, V - 1]), rng.permutation(np.arange(1, V - 1))]); b[1:4] = True
    st = np.flatnonzero(b); en = np.append(st[1:], V) - 1; T = len(st); top = o[st]; last = o[en]
    par = np.empty(V, np.int64); side = np.zeros(V, np.int64); kd = np.full(V, W, np.int64)
    par[o[1:]] = o[:-1]
    w = rng.permutation(T); gp = rng.permutation(S); n = min((T + 1) // 2, int(rng.integers(S // 2, S + 1)), most)
    if ends: w = np.concatenate([np.array([0, 1]), 2 + rng.permutation(T - 2)]); gp = np.concatenate([np.array([0, S - 1]), 1 + rng.permutation(S - 2)])
    par[top[w[:n]]] = V + gp[:n]; side[top[w[:n]]] = rng.integers(0, 2, n)
    c = w[n:]; z = rng.random(len(c)) < ring
    par[top[c[z]]] = last[c[z]]
    e = c[~z]; v = rng.permutation(V)
    if ends:
        for i in range(min(4, len(e))):
            j = int(np.flatnonzero(v == top[e[i]])[0]); h = v[i]; v[i] = v[j]; v[j] = h
    v = v[:len(e)]; par[top[e]] = v; side[top[e]] = 1; kd[v] = top[e]
    return par, side, kd
def pairs(rng, share, coin, classes=False):
    h = V // 2; o = rng.permutation(V)
    if classes: o = o[np.argsort(-((o - int(rng.integers(0, 16))) % 16), kind="stable")]; o[:h] = rng.permutation(o[:h])
    a, f = o[:h], o[h:]; b = rng.random(h) < share; b[0] = True
    st = np.flatnonzero(b); en = np.append(st[1:], h) - 1; T = len(st)
    par = np.empty(V, np.int64); side = np.zeros(V, np.int64); kd = np.full(V, W, np.int64)
    par[a[1:]] = a[:-1]; par[f] = a
    mid = np.ones(h, bool); mid[en] = False; j = np.flatnonzero(mid); c = rng.random(len(j)) < coin
    side[f[j]] = np.where(c, 0, 1); side[a[j + 1]] = np.where(c, 1, 0); kd[a[j]] = np.where(c, a[j + 1], f[j])
    w = rng.permutation(T); n = min((T + 1) // 2, int(rng.integers(S // 2, S + 1))); top = a[st]
    side[top] = 1; par[top[w[:n]]] = V + rng.permutation(S)[:n]; side[top[w[:n]]] = rng.integers(0, 2, n)
    e = a[en][rng.permutation(T)[:T - n]]; par[top[w[n:]]] = e; kd[e] = top[w[n:]]
    return par, side, kd, a, f
def comb(rng, T):
    R = 8; m = min(D, 5); n = T - R; q = V - R * m; big = min(n, (q - 2 * n) // (D - 2)); rest = q - 2 * n - big * (D - 2)
    ln = np.full(n, 2, np.int64); ln[:big] = D
    if big < n: ln[big] += rest; rest = 0
    ln = np.concatenate([np.full(R, m, np.int64), rng.permutation(ln), np.ones(rest, np.int64)])
    o = rng.permutation(V); en = np.add.accumulate(ln) - 1; top = o[en - ln + 1]; last = o[en]
    par = np.empty(V, np.int64); side = np.zeros(V, np.int64); kd = np.full(V, W, np.int64)
    par[o[1:]] = o[:-1]
    free = np.ones(V, bool); free[o[:R * m]] = False; free[last[:T]] = False; a = rng.permutation(np.flatnonzero(free))
    par[top[:R]] = last[:R]; side[top[:R]] = 1; kd[last[:R]] = top[:R]
    t = rng.permutation(top[R:]); w = int(rng.integers(S // 2, S + 1))
    par[t[:w]] = V + rng.permutation(S)[:w]; side[t[:w]] = rng.integers(0, 2, w)
    e = t[w:]; v = a[:len(e)]; par[e] = v; side[e] = 1; kd[v] = e
    off = np.zeros(V, np.int64); off[last[:T]] = 4
    for k in range(1, m): off[o[en[:R] - k]] = max(0, 4 - (m - k))
    sg = np.empty((16, V), np.int64); sg[:, o] = np.repeat(2 * rng.integers(0, 2, (16, len(ln))) - 1, ln, axis=1)
    return par, side, kd, a, np.where(free[None, :], rng.integers(0, 2, (16, V)), sg * off[None, :])
def knit(z):
    return [np.stack([np.stack([z[q][g][i] for g in range(8)]) for q in range(N)]) for i in range(3)]
def shown(rng):
    return np.ascontiguousarray(np.argsort(rng.random((N, 8, V)), axis=-1)[..., :S]).reshape(N, 8, N - 1, G)
def seen(x, sl):
    z = []
    for r in range(N):
        w = [x[r]]
        for d in range(1, N):
            q = (r - d) % N; w.append(np.take_along_axis(x[q], sl[q][:, d - 1][:, None, :], 2))
        z.append(np.concatenate(w, axis=2))
    return np.stack(z)
def gaps(full, par):
    return np.add.reduce(np.abs(full[..., :V] - np.take_along_axis(full, par[:, :, None, :], 3)), axis=2)
def level(v, share):
    s = np.sort(v, axis=-1); n = v.shape[-1]; i = np.clip(((1 - share) * n).astype(np.int64), 0, n - 1)
    return np.take_along_axis(s, i[..., None], 2)[..., 0]
def numbers16(rng):
    u = rng.random((N, 8, 16, V)) ** np.exp2(rng.integers(-1, 2, (N, 8, 1, V)))
    return np.minimum(np.floor(16 * u), 15).astype(np.int64)
def pack(x, par, side, kd, sl, th, A):
    return {"x": np.ascontiguousarray(x.reshape(N, 128, V)).astype(np.float32).astype(BF), "hang": np.stack([gtable(a) for a in 2 * par + side]), "kid": np.stack([gtable(a) for a in kd]),
            "shw": np.stack([gtable(a.reshape(8, -1)) for a in sl]), "bar": np.repeat(np.stack([th, A], axis=-1), 16, axis=1).astype(np.int32)}
def setup_inputs(rng):
    sh = rng.choice(np.array([0.15, 0.25, 0.4]), (N, 8))
    par, side, kd = knit([[weave(rng, sh[q, g]) for g in range(8)] for q in range(N)]); sl = shown(rng); x = numbers16(rng)
    th = level(gaps(seen(x, sl), par), rng.choice(np.array([0.1, 0.2, 0.35, 0.6]), (N, 8)))
    A = level(np.add.reduce(x, axis=2), rng.choice(np.array([0.02, 0.08, 0.2]), (N, 8)))
    return pack(x, par, side, kd, sl, th, A)
def setup_inputs_room(rng):
    h = V // 2; b = rng.integers(4, 12, (8, 16, 1)); th = rng.integers(8, 41, (N, 8))
    A = np.add.reduce(b[:, :, 0], axis=1)[None, :] + rng.choice(np.array([0, 1, 1, 16]), (N, 8))
    x = np.empty((N, 8, 16, V), np.int64); sl = np.empty((N, 8, N - 1, G), np.int64); z = []
    for q in range(N):
        z.append([])
        for g in range(8):
            k = pairs(rng, 0.3, 0.5, g > 5); z[q].append(k); a, f = k[3], k[4]
            sl[q, g] = rng.permutation(a)[:S].reshape(N - 1, G)
            n = int(rng.choice(np.array([0, 1, L - 1, L, L + 1, h])))
            if q < 2: n = (L, L + 1, h, L - 1, 1, 0, L, L + 1)[(g + q) % 8]
            t0 = int(th[q, g]); coin = rng.random(h) < 0.5; hit = (np.arange(h) if g > 5 else rng.permutation(h)) < n
            t = np.where(hit, np.where(coin, t0, rng.integers(t0, 64, h)), np.where(coin, t0 - 1, rng.integers(0, t0, h)))
            size = (t[None, :] + (np.arange(16)[:, None] + rng.integers(0, 16, h)[None, :]) % 16) // 16
            v = np.repeat(b[g], V, axis=1); v[:, f] = b[g] + size * (2 * rng.integers(0, 2, (16, h)) - 1); x[q, g] = v
    par, side, kd = knit(z)
    return pack(x, par, side, kd, sl, th, A)
def setup_inputs_deep(rng):
    few = min(L, -(-V // D)); z = []
    for q in range(N): z.append([weave(rng, 0.04, 0.3) if g % 4 == 0 else pairs(rng, 0.02, 0.0) if g % 4 == 1 else comb(rng, L if g % 4 == 2 else few) for g in range(8)])
    par, side, kd = knit(z); sl = shown(rng); x = numbers16(rng); b = rng.integers(4, 12, (8, 16, 1))
    for q in range(N):
        for g in (2, 3, 6, 7):
            x[q, g] = b[g] + z[q][g][4]; sl[q, g] = rng.permutation(z[q][g][3])[:S].reshape(N - 1, G)
    th = level(gaps(seen(x, sl), par), rng.choice(np.array([0.03, 0.06, 0.1]), (N, 8)))
    th[:, np.array([2, 3, 6, 7])] = rng.integers(17, 49, (N, 4))
    return pack(x, par, side, kd, sl, th, np.full((N, 8), 255))
def setup_inputs_ends(rng):
    par, side, kd = knit([[weave(rng, 0.3, 0.2, True) for g in range(8)] for q in range(N)]); sl = np.empty((N, 8, N - 1, G), np.int64)
    for q in range(N):
        for g in range(8): sl[q, g] = np.concatenate([np.array([0]), rng.permutation(np.arange(1, V - 1))[:S - 2], np.array([V - 1])]).reshape(N - 1, G)
    x = np.repeat(15 * rng.integers(0, 2, (N, 8, 1, V)), 16, axis=2)
    odd = (rng.random((N, 8, 1, V)) < 0.3) & (np.arange(16)[:, None] == rng.integers(0, 16, (N, 8, 1, V)))
    x = np.where(odd, np.abs(x - 1), x)
    th = rng.choice(np.array([0, 1, 239, 240, 241]), (N, 8)); A = rng.choice(np.array([0, 1, 239, 240, 241, 255]), (N, 8))
    th[0] = np.array([0, 1, 239, 240, 240, 0, 239, 1]); A[0] = np.array([241, 240, 239, 241, 0, 1, 241, 240])
    return pack(x, par, side, kd, sl, th, A)
def setup_inputs_afar(rng):
    sh = rng.choice(np.array([0.2, 0.3, 0.4]), (N, 8))
    par, side, kd = knit([[weave(rng, sh[q, g]) for g in range(8)] for q in range(N)]); sl = shown(rng)
    for q in range(N):
        sl[q, 1] = ((V // 16) * int(rng.integers(0, 9)) + rng.permutation(S)).reshape(N - 1, G)
        v = np.argsort((np.arange(V) - int(rng.integers(0, 16))) % 16, kind="stable")[:S]; sl[q, 4] = rng.permutation(v).reshape(N - 1, G)
    b = np.empty((N, 8, 16, 1), np.int64)
    for g in range(8):
        o = rng.permutation(16)
        for q in range(N): b[q, g, :, 0] = [13 if bin(int(i) & (q + 1)).count("1") % 2 else 2 for i in o]
    x = b + rng.integers(0, 2, (N, 8, 16, V))
    th = rng.choice(np.array([17, 40, 80, 90]), (N, 8)); th[rng.integers(0, N, 8), np.arange(8)] = rng.integers(242, 256, 8)
    return pack(x, par, side, kd, sl, th, rng.choice(np.array([128, 255, 255]), (N, 8)))
def setup_inputs_spread(rng):
    sh = 0.02 + 0.6 * rng.random((N, 8)); full = np.arange(8) % 3 == 2
    par, side, kd = knit([[weave(rng, 0.9, 0.0, False, 16) if full[g] else weave(rng, sh[q, g], 0.1) for g in range(8)] for q in range(N)]); sl = shown(rng)
    x = np.minimum(np.floor(np.exp2(4 * rng.random((N, 8, 1, V))) * (0.05 + rng.random((N, 8, 16, V)))), 15).astype(np.int64)
    th = level(gaps(seen(x, sl), par), np.where(full, 0.15, np.exp2(-6 * rng.random((N, 8)))))
    A = np.where((rng.random((N, 8)) < 0.7) | full, level(np.add.reduce(x, axis=2), np.where(full, 0.03, np.exp2(-6 * rng.random((N, 8))))), rng.integers(0, 256, (N, 8)))
    return pack(x, par, side, kd, sl, th, A)
def check_inputs(d):
    bad = []; x = np.asarray(d["x"]).astype(np.float32)
    if not np.all((x >= 0) & (x <= 15) & (x == np.floor(x))): bad.append("range of x")
    for k, lo, hi in (("hang", 0, 2 * W - 1), ("kid", 0, W), ("shw", 0, V - 1), ("bar", 0, 255)):
        if np.min(d[k]) < lo or np.max(d[k]) > hi: bad.append("range of " + k)
    b = np.asarray(d["bar"]).reshape(N, 8, 16, 2)
    if np.any(b != b[:, :, :1]): bad.append("bar not alike on a group's rows")
    if bad: return bad
    for r in range(N):
        hs, ks, ss = (gentries(np.asarray(d[k][r])).astype(np.int64) for k in ("hang", "kid", "shw"))
        for g in range(8):
            h = hs[g]; p = h >> 1; own = p < V
            if len(np.unique(h[own])) < np.count_nonzero(own): bad.append("two stitches on one side of a parent")
            if len(np.unique(p[~own])) < np.count_nonzero(~own): bad.append("two stitches under one ghost")
            m = np.flatnonzero(own & (h % 2 == 1)); want = np.full(V, W, np.int64); want[p[m]] = m
            if np.any(ks[g] != want): bad.append("kid against hang")
            if len(np.unique(ss[g])) < S: bad.append("a stitch shown twice")
    return sorted(set(bad))
def reference(x, hang, kid, shw, bar):
    now = x.astype(np.float32).astype(np.int64).reshape(N, 8, 16, V)
    h = np.stack([gentries(a) for a in hang]).astype(np.int64); par = h >> 1; side = h & 1
    kd = np.stack([gentries(a) for a in kid]).astype(np.int64); sl = np.stack([gentries(a) for a in shw]).astype(np.int64).reshape(N, 8, N - 1, G)
    th = bar[:, ::16, 0].astype(np.int64); A = bar[:, ::16, 1].astype(np.int64)
    flag = np.zeros((N, 8, V), bool)
    for rnd in range(RO):
        full = seen(now, sl)
        cand = (gaps(full, par) >= th[:, :, None]) | flag
        drop = cand & (np.add.accumulate(cand.astype(np.int64), axis=2) <= L)
        stop = np.ones((N, 8, W), bool); stop[..., :V] = drop | (np.add.reduce(now, axis=2) >= A[:, :, None])
        slot = np.zeros((N, 8, W), bool); now = now.copy(); par2 = par.copy(); side2 = side.copy(); kd2 = kd.copy()
        for r in range(N):
            for g in range(8):
                p, s, c1, st, f = par[r, g], side[r, g], kd[r, g], stop[r, g], full[r, g]
                p2, s2, c2, new = par2[r, g], side2[r, g], kd2[r, g], now[r, g]
                d = [np.flatnonzero(drop[r, g])]; live = [np.ones(len(d[0]), bool)]
                top = np.full(len(d[0]), W, np.int64)
                for k in range(D):
                    i = np.flatnonzero(live[k]); v = d[k][i]; u = p[v]
                    nxt = d[k].copy(); nxt[i] = u; go = np.zeros(len(nxt), bool); go[i] = (s[v] == 0) & ~st[u]
                    top[i] = c1[v]; d.append(nxt); live.append(go)
                anchor = d[D]; slot[r, g][anchor[anchor >= V]] = True
                up = f[:, anchor]
                for k in range(D - 1, -1, -1):
                    up = (f[:, d[k]] + up) >> 1
                    new[:, d[k][live[k]]] = up[:, live[k]]
                for k in range(D):
                    i = np.flatnonzero(live[k]); v = d[k][i]
                    if k == 0:
                        c = top[i]; has = c < V; c2[v] = c; p2[c[has]] = v[has]; s2[c[has]] = 1
                    else:
                        w = d[k - 1][i]; c = c1[w]; has = c < V
                        c2[v] = np.where(has, w, W); p2[c[has]] = v[has]; s2[c[has]] = 0; s2[w[has]] = 1
        par, side, kd = par2, side2, kd2
        flag = np.zeros((N, 8, V), bool)
        for q in range(N):
            for e in range(1, N):
                r = (q + e) % N; z = slot[r, :, V + (e - 1) * G:V + e * G]
                for g in range(8): flag[q, g][sl[q, g, e - 1][z[g]]] = True
    return {"y": now.reshape(N, 128, V).astype(np.float32).astype(BF), "yh": (2 * par + side).astype(np.float32)}

from concourse.bass import DstId, RemoteDMATransfer
from concourse.mybir import AluOpType, ActivationFunctionType

A, F = AluOpType, ActivationFunctionType
V, S, L, W = 3072, 448, 768, 3520
OFF = 136.0
CST = 412
MAG = 12582912.0
BF, F32, I32, U16 = "bfloat16", "float32", "int32", "uint16"
PATS = ["ONE", "W224", "W2", "W16", "M4K", "A0", "A1", "B0", "B1", "B2", "B3", "KD", "FLP", "DH"]
TUNE = {"ev": (2, 2), "x": (1024, 1024), "st": (1152, 1536), "sp": (1792, 1536)}
SCRATCH = {}
for _names, _n, _dt in (
        ("X0 X1 X2", W + V, BF), ("XL D", V, BF), ("ST", W + 16, BF), ("G", 5 * L, BF), ("AT", 3584 + L, BF),
        ("GA", 2 * L, BF), ("C", 16 * CST, BF), ("CW", V + 192, BF), ("CS CMP", L, BF), ("SL F2", V, F32),
        ("WW", 3584 + L, F32), ("FW0 FW1", L + S, F32), ("LF0 LF1", S, F32), ("SD0 SD1 SD2", S, BF), ("JR", L, F32),
        ("PAT", 144 * len(PATS), BF), ("E", 144, BF), ("BLK TLE TGT TMPM", 128, BF), ("ID", 1024, BF),
        ("IDF GROW", 128, F32), ("NROW VN HF CAP T4 HK GDL T1 T2 T3 CUM BASE FL THL NT THR", 192, F32),
        ("HI PI Q QA QB HKI KI", 192, I32), ("G5 F5", 240, I32), ("EE", 240, F32), ("ZF WL", 224, F32),
        ("LHI LLO LSD LHK LHV LDR", 224, BF), ("C0 C1 C2 C3", CST, BF), ("CAND DRP TB CIO", 192, BF), ("SS", 208, BF),
        ("OP OQ OX OC", 192, U16), ("OA OG", 240, U16), ("OS OSP OCS", 32, U16), ("OCJ OAN", 48, U16),
        ("SHI SH1 SH2", 32, I32), ("SHF SHG DJ D12 T48 U48", 48, F32), ("COL WC RR", 16, F32), ("PC BARI", 8, I32),
        ("TT", 256, F32)):
    for _nm in _names.split():
        SCRATCH[_nm] = ("sbuf", [128, _n], _dt)
for _i in range(8):
    SCRATCH["P%d" % _i] = ("psum", [128, 512], F32)
SEMAPHORES = ["sV", "sS", "sT", "sG", "sent"] + ["ar%d" % i for i in range(5)] + ["d%d" % i for i in range(48)]


def engine_split(src, dsts, topo):
    far = [d for d in dsts if topo.chip(d) != topo.chip(src)]
    near = [d for d in dsts if topo.chip(d) == topo.chip(src)]
    out, used = {}, []
    pool = topo.engines(src, far[0])
    spare = len(pool) - len(far)
    for d in far:
        take = 2 if spare > 0 else 1
        spare -= take - 1
        e = [x for x in topo.engines(src, d) if x not in used][:take]
        used.extend(e)
        out[d] = e
    for d in near:
        e = [x for x in topo.engines(src, d) if x not in used and x not in pool][:2]
        used.extend(e)
        out[d] = e
    return out


def rank_program(g, core, T, topo):
    rank = T.rank_of(core)
    if rank is None:
        return
    cores = list(T.cores)
    N = len(cores)
    ops = []

    def R(nm, a=None, b=None, step=1, row=None, parts=None):
        n = SCRATCH[nm][1][1]
        a = 0 if a is None else a
        b = n if b is None else b
        if row is not None:
            p = T[nm][row:128:16, a:b]
        elif parts is not None:
            p = T[nm][0:parts, a:b]
        elif step != 1:
            p = T[nm][:, a:b:step]
        else:
            p = T[nm][:, a:b]
        if SCRATCH[nm][0] == "psum":
            return (p, [(nm, 0, 512, None, True)])
        return (p, [(nm, a, b, row, False)])

    def IND(w, o):
        return (w[0].indirect(o[0]), w[1], o[1])

    def X(p):
        return (p, [])

    def ap(x):
        return x[0] if isinstance(x, tuple) else x

    def add(e, fn, out, ins, grp=None):
        reads = []
        for x in ins:
            if isinstance(x, tuple):
                for part in x[1:]:
                    reads.extend(part)
        if len(out) == 3:
            reads = reads + out[2]
        ops.append({"e": e, "fn": fn, "w": list(out[1]), "r": reads, "grp": grp})

    def ts(out, i, s1, o0, s2=None, o1=None):
        if o1 is None:
            add("V", lambda: g.vector.tensor_scalar(out[0], i[0], ap(s1), None, o0), out, (i, s1))
        else:
            add("V", lambda: g.vector.tensor_scalar(out[0], i[0], ap(s1), ap(s2), o0, o1), out, (i, s1, s2))

    def tt(out, a, b, o):
        add("V", lambda: g.vector.tensor_tensor(out[0], a[0], b[0], o), out, (a, b))

    def cp(out, i):
        add("V", lambda: g.vector.tensor_copy(out[0], i[0]), out, (i,))

    def ms(out, c):
        add("V", lambda: g.vector.memset(out[0], c), out, ())

    def scan(out, a, b, o0, o1):
        add("V", lambda: g.vector.tensor_tensor_scan(out[0], a[0], b[0], 0.0, o0, o1), out, (a, b))

    def act(out, i, f=None, bias=0.0, scale=1.0):
        if f is None:
            add("S", lambda: g.scalar.activation(out[0], i[0], F.Identity, bias=ap(bias), scale=ap(scale)), out, (i, bias, scale))
        elif f == F.Relu or f == F.Abs:
            add("S", lambda: g.scalar.activation(out[0], i[0], f, bias=bias, scale=scale), out, (i,))
        else:
            add("S", lambda: g.scalar.activation(out[0], i[0], f), out, (i,))

    def mm(out, l, r, st, sp):
        add("T", lambda: g.tensor.matmul(out[0], l[0], r[0], st, sp), out, (l, r))

    def iota(out, pat, base, cm, small=True):
        if small:
            add("G", lambda: g.iota(out[0], pat, base, cm, allow_small_or_imprecise_dtypes=True), out, ())
        else:
            add("G", lambda: g.iota(out[0], pat, base, cm), out, ())

    groups = {}

    def dma(out, i, grp=None, q="Y"):
        grp = grp or "n%d" % len(ops)
        if grp not in groups:
            groups[grp] = ["d%d" % len(groups), 0]
        groups[grp][1] += 16
        eng = g.sync if q == "Y" else g.scalar
        add(q, lambda: eng.dma_start(out[0], i[0]), out, (i,), grp=grp)

    def rl(out, pat, nm, a, n, first=True, last=True):
        o = 144 * PATS.index(pat) + 15
        for i in range(16):
            mm(out, R("PAT", o - i, o - i + 128), R(nm, a + i, a + n, 16), first and i == 0, last and i == 15)

    peers = [cores[(rank + b + 1) % N] for b in range(N - 1)]
    mine = engine_split(core, peers, topo)
    arrive = 0
    for p in peers:
        pr = cores.index(p)
        arrive += len(engine_split(p, [cores[(pr + b + 1) % N] for b in range(N - 1)], topo)[core])
    sent = [0]

    def exchange(k, src, s0, dst, d0):
        def fn():
            tr = []
            for b, p in enumerate(peers):
                rid, pid, _ = topo.addr(p)
                m = 0
                for e in mine[p]:
                    m += 1 << e
                bb = N - 2 - b
                tr.append(RemoteDMATransfer(dst_ids=[DstId(rid=rid, pnc=pid)], dma_engine_mask=m, remote_sem=T.sem["ar%d" % k],
                                            src=T[src][:, s0 + 64 * b:s0 + 64 * b + 64], dst=T[dst][:, d0 + 64 * bb:d0 + 64 * bb + 64]))
            return g.remote_dma_fused(tr, local_sem=T.sem.sent)
        sent[0] += sum(len(v) for v in mine.values())
        ops.append({"e": "G", "fn": fn, "w": [], "r": R(src, s0, s0 + S)[1], "grp": "remote"})
        groups["ar%d" % k] = ["ar%d" % k, arrive]
        ops.append({"e": "X", "fn": None, "w": R(dst, d0, d0 + S)[1], "r": [], "grp": "ar%d" % k})

    def col(nm, j):
        return R(nm, j, j + 1)

    def split(out_nm, o0, win, offs, n, nv, bias=0.0):
        if bias:
            ts(R(out_nm, o0, o0 + nv), IND(win, R(offs, 0, nv // 16)), bias, A.add)
        else:
            cp(R(out_nm, o0, o0 + nv), IND(win, R(offs, 0, nv // 16)))
        act(R(out_nm, o0 + nv, o0 + n), IND(win, R(offs, nv // 16, n // 16)), bias=bias)

    dma(R("SHI", 0, 28), X(T.shw[:]))
    dma(R("XL", 0, 1536), X(T.x[:, 0:1536]), "x")
    dma(R("XL", 1536, V), X(T.x[:, 1536:V]), "x", q="S")
    dma(R("HI"), X(T.hang[:]), "hk", q="S")
    dma(R("KI"), X(T.kid[:]), "hk")
    dma(R("BARI", 0, 2), X(T.bar[:]), "hk")
    iota(col("PC", 0), [[1, 1]], 0, 1, False)
    iota(R("NROW"), [[1, 192]], 0, 0)
    iota(R("GROW"), [[1, 8], [0, 16]], 0, 0)
    iota(R("VN"), [[16, 192]], 0, 1)
    ms(R("AT"), 1.0)
    ts(col("PC", 1), col("PC", 0), 4, A.arith_shift_right)
    ts(col("PC", 2), col("PC", 0), 15, A.bitwise_and)
    cp(R("COL", 0, 3), R("PC", 0, 3))
    ts(col("COL", 3), col("COL", 1), 16.0, A.mult, 15.0, A.add)
    ts(col("COL", 4), col("COL", 1), -16.0, A.mult)
    ts(R("E"), R("NROW", 0, 144), col("COL", 3), A.is_equal)
    ts(R("RR", 0, 8), R("NROW", 0, 8), col("COL", 2), A.is_equal)
    cp(R("OS", 0, 28), R("SHI", 0, 28))
    ts(R("SD0"), IND(R("XL"), R("OS", 0, 28)), OFF, A.add)
    exchange(0, "SD0", 0, "X0", V)
    iota(R("JR"), [[1, L]], 0, 0)
    iota(R("SL"), [[1, V]], W, 0)
    iota(R("C"), [[0, 16 * CST]], 0, 0)
    iota(R("FW0", L), [[0, S]], 0, 0)
    iota(R("FW1", L), [[0, S]], 0, 0)

    def rr(j):
        return col("RR", j)

    def wc(j):
        return col("WC", j)

    def pat(nm, sc):
        o = 144 * PATS.index(nm)
        act(R("PAT", o, o + 144), R("E"), scale=sc)

    def fill(out, c):
        n = out[1][0][2] - out[1][0][1]
        act(out, R("NROW", 0, n), scale=0.0, bias=c)
    pat("ONE", 1.0)
    fill(R("ZF", 0, 112), 0.0)
    fill(R("ZF", 112, 224), 0.0)
    act(R("VN"), R("VN"), bias=col("COL", 4))
    act(R("X0", 1792, V), R("XL", 1792, V), bias=OFF)
    ts(R("X0", 0, 1792), R("XL", 0, 1792), OFF, A.add)
    rl(R("P1", 0, 192), "ONE", "X0", 0, V)
    ts(R("QA"), R("HI"), 7, A.arith_shift_right)
    ts(R("T1"), R("QA"), -256.0, A.mult, 768.0 + 256.0 * 48, A.add)
    ts(R("T2"), R("QA"), 48.0, A.is_ge)
    tt(R("GDL"), R("T1"), R("T2"), A.mult)
    tt(R("HI"), R("HI"), R("GDL"), A.add)
    ts(R("PI"), R("HI"), 1, A.arith_shift_right)
    cp(R("OP"), R("PI"))
    cp(R("HF"), R("HI"))
    ts(R("HK"), R("KI"), float(W), A.is_lt)
    cp(R("COL", 5, 7), R("BARI", 0, 2))
    ts(col("COL", 7), col("COL", 6), 16 * OFF, A.add)
    ts(R("BLK"), R("GROW"), col("COL", 1), A.is_equal)
    ts(R("TMPM"), R("NROW", 0, 128), col("COL", 0), A.is_ge)
    tt(R("TLE"), R("TMPM"), R("BLK"), A.mult)
    tt(R("TGT"), R("BLK"), R("TLE"), A.subtract)
    ts(R("IDF"), R("NROW", 0, 128), col("COL", 0), A.is_equal)
    dma(R("WW", 0, 3584, row=0), R("ZF"))
    dma(R("F2", row=0), R("ZF", 0, 192))
    for nm in ("LHI", "LLO", "LSD", "LHK", "LHV", "LDR"):
        fill(R(nm, 192, 224), 1.0)
    pat("M4K", -4096.0)
    pat("W224", 224.0)
    pat("W2", 2.0)
    pat("W16", 0.0625)
    act(R("ID", 512, 640), R("IDF"), scale=-4096.0)
    act(R("ID", 640, 768), R("IDF"))
    act(R("ID", 768, 896), R("IDF"), scale=-1.0)
    act(R("ID", 896, 1024), R("IDF"), scale=16384.0)
    act(R("CIO"), R("NROW"))
    act(R("D12", 0, 12), R("VN", 0, 12), bias=float(V))
    fill(R("SS", 0, 16), 0.0)

    def setup_late():
        act(wc(12), rr(4), bias=rr(6))
        act(wc(0), rr(1), scale=224.0, bias=rr(0))
        act(wc(3), rr(0), scale=32.0, bias=rr(3))
        act(wc(10), rr(0), scale=2.0)
        act(wc(1), rr(2), scale=8192.0, bias=wc(0))
        act(wc(4), rr(1), scale=2.0, bias=wc(3))
        act(wc(11), rr(1), scale=2.0, bias=wc(10))
        act(wc(2), wc(12), scale=8192.0, bias=wc(1))
        act(wc(5), rr(5), scale=16384.0, bias=wc(4))
        act(wc(6), wc(12), scale=-131072.0, bias=wc(4))
        for k in (1, 2, 3):
            act(wc(6 + k), rr(5), scale=16384.0 * (k + 1), bias=wc(6))
        act(R("DJ"), R("VN", 0, 48), bias=3584.0)
        for nm, j in (("A0", 1), ("B0", 5), ("A1", 2), ("B1", 7), ("B2", 8), ("B3", 9), ("KD", 11)):
            pat(nm, wc(j))
        pat("FLP", rr(2))
        pat("DH", rr(3))
        for k in range(4):
            act(R("ID", 128 * k, 128 * k + 128), R("IDF"), scale=0.5 ** (k + 1))
        act(R("U48"), R("VN", 0, 48), bias=float(V - L))
        fill(R("ST", 0, 16), 0.0)
        for a in (0, 192, 384):
            fill(R("ST", V + 16 + a, min(V + 208 + a, W + 16)), 0.0)
        fill(R("NT", 144, 192), 0.0)
        for k in range(3):
            fill(R("THR", 48 * k, 48 * k + 48), 16384.0 * (k + 2))
        fill(R("EE", 0, 48), 0.0)
        for nm in ("C0", "C1", "C2", "C3"):
            fill(R(nm, 0, 192), 0.0)
            fill(R(nm, 192, 220), 0.0)

    def shown_places():
        ts(R("SH1", 0, 28), R("SHI", 0, 28), 15, A.bitwise_and)
        ts(R("SH2", 0, 28), R("SHI", 0, 28), 4, A.arith_shift_right)
        ts(R("SHF", 0, 28), R("SH1", 0, 28), 192.0, A.mult)
        tt(R("SHG", 0, 28), R("SHF", 0, 28), R("SH2", 0, 28), A.add)
        cp(R("OSP", 0, 28), R("SHG", 0, 28))

    def attr(j, gname):
        nm = ("LHI", "LLO", "LSD", "LHK", "", "", "LHV")[j]
        if j == 0:
            ts(R("QA"), R("HI"), 5, A.arith_shift_right)
            cp(R(nm, 0, 192), R("QA"))
        elif j == 1:
            ts(R("QB"), R("HI"), 1, A.arith_shift_right, 15, A.bitwise_and)
            cp(R(nm, 0, 192), R("QB"))
        elif j == 2:
            ts(R("Q"), R("HI"), 1, A.bitwise_and)
            cp(R(nm, 0, 192), R("Q"))
        elif j == 3:
            act(R(nm, 0, 192), R("HK"))
        else:
            ts(R(nm, 0, 192), R("P1", 0, 192), col("COL", 7), A.is_ge)
        dma(R("AT", 0, 3584, row=j), R(nm), gname)

    for j in (0, 1, 2, 3, 6):
        attr(j, "at0")
    shown_places()

    def lv(nm, k):
        return R(nm, 48 * k, 48 * k + 48)

    def frozen(k):
        ts(lv("F5", k), lv("G5", k), 16383, A.bitwise_and, 1, A.arith_shift_right)
        cp(lv("OG", k), lv("F5", k))

    for r in range(3):
        Xr, last, gat = "X%d" % r, r == 2, "at%d" % r
        act(R("D", 2560, V), IND(R(Xr, 0, W), R("OP", 160, 192)))
        mm(R("P3"), R("ID", 640, 768), R("D", 2560, V), True, False)
        mm(R("P3"), R("ID", 768, 896), R(Xr, 2560, V), False, True)
        act(R("D", 2560, V), R("P3"), F.Abs)
        rl(R("P0", 160, 192), "ONE", "D", 2560, 512)
        for a, b in ((0, 1024), (1024, 1792), (1792, 2304), (2304, 2560)):
            tt(R("D", a, b), IND(R(Xr, 0, W), R("OP", a // 16, b // 16)), R("XL", a, b), A.subtract)
            act(R("D", a, b), R("D", a, b), F.Abs, bias=-OFF if r == 0 else 0.0)
            rl(R("P0", a // 16, b // 16), "ONE", "D", a, b - a)
        ms(R("CW", 0, L), 0.0)
        if r > 0:
            tt(R("HK"), R("P2", 0, 192), R("HK"), A.add)
            cp(R("HI"), R("HF"))
            act(R("THL"), R("FL"), scale=-1.0, bias=col("COL", 5))
            attr(6, gat)
            attr(3, gat)
            attr(0, gat)
            tt(R("CAND"), R("P0", 0, 192), R("THL"), A.is_ge)
        else:
            ts(R("CAND"), R("P0", 0, 192), col("COL", 5), A.is_ge)
        scan(R("SS", 16, 208), R("CAND"), R("CAND"), A.add, A.max)
        rl(R("P2", 0, 12), "M4K", "CAND", 0, 192)
        rl(R("P3", 0, 12), "ONE", "SS", 15, 192)
        mm(R("P5", 0, 192), R("TLE"), R("SS", 16, 208), True, False)
        mm(R("P5", 0, 192), R("TGT"), R("SS", 15, 207), False, False)
        mm(R("P5", 0, 192), R("ID", 512, 640), R("CAND"), False, True)
        mm(R("P4", 0, 192), R("TLE"), R("SS", 16, 208), True, False)
        mm(R("P4", 0, 192), R("TGT"), R("SS", 15, 207), False, True)
        act(R("LDR", 0, 192), R("P5", 0, 192), F.Relu, bias=float(L + 1 - 4096), scale=-1.0)
        dma(R("AT", 0, 3584, row=4), R("LDR"))
        act(R("CUM"), R("P4", 0, 192))
        act(R("DRP"), R("LDR", 0, 192), F.Sign)
        act(R("T4"), R("CUM"), bias=float(W - 1))
        if r > 0:
            attr(1, gat)
        tt(R("T48", 0, 12), R("P2", 0, 12), R("D12", 0, 12), A.add)
        tt(R("T48", 16, 28), R("P3", 0, 12), R("T48", 0, 12), A.max)
        cp(R("OCS", 0, 12), R("T48", 16, 28))
        cp(IND(R("CW"), R("OCS", 0, 12)), R("CIO"))
        scan(R("CS"), R("CW", 0, L), R("CW", 0, L), A.max, A.max)
        rl(R("P6", 0, 48), "W16", "CS", 0, L)
        rl(R("P7", 0, 48), "W16", "CS", 0, L, True, False)
        rl(R("P5", 0, 48), "W2", "CS", 0, L, True, False)
        if r > 0:
            attr(2, gat)
        else:
            setup_late()
        cp(R("OCJ"), R("P6", 0, 48))
        tt(R("CMP"), IND(R("CUM"), R("OCJ")), R("JR"), A.is_le)
        rl(R("P7", 0, 48), "W224", "CMP", 0, L, False, True)
        rl(R("P5", 0, 48), "W2", "CMP", 0, L, False, True)
        tt(R("TB"), R("DRP"), R("LHV", 0, 192), A.add)
        act(R("CAP"), R("TB"), scale=-8192.0, bias=8192.0)
        mm(R("P0", 0, 192), R("IDF"), R("HF"), True, False)
        mm(R("P0", 0, 192), R("ID", 896, 1024), R("LSD", 0, 192), False, True)
        tt(R("T3"), R("T4"), R("DRP"), A.mult)
        cp(R("OA", 0, 48), R("P7", 0, 48))
        for k in range(4):
            ga = (k % 2) * L
            cp(R("GA", ga, ga + L), IND(R("AT"), lv("OA", k)))
            if k < 3:
                rl(R("P6", 0, 48), "A0" if k == 0 else "A1", "GA", ga, L)
            if k == 0:
                cp(lv("G5", 0), R("P5", 0, 48))
            else:
                tt(lv("G5", k), R("P7", 0, 48), lv("G5", k - 1), A.max)
            frozen(k)
            rl(R("P7", 0, 48), "B%d" % k, "GA", ga, L)
            if k == 0:
                act(R("G", 0, L), IND(R(Xr, 0, W), lv("OG", 0)))
                tt(R("BASE"), R("T3"), R("VN"), A.max)
                ts(R("OQ"), R("P0", 0, 192), 0.5, A.mult, 15.5 - 8192.0, A.add)
            else:
                cp(R("G", L * k, L * k + L), IND(R(Xr, 0, W), lv("OG", k)))
            if k < 3:
                tt(R("T48"), R("P6", 0, 48), R("DJ"), A.min)
                cp(lv("OA", k + 1), R("T48"))
                act(IND(R("WW"), lv("OA", k + 1)), R("SL", L * (k + 1), L * (k + 2)), F.Silu)
        dma(R("WL"), R("WW", 0, 3584, row=0))
        if not last:
            dma(R("WW", 0, 3584, row=0), R("ZF"))
        fin = []
        for b in range(6):
            c0 = 512 * b
            mm(R("P%d" % b), R("ID", 0, 128), R("G", c0, c0 + 512), True, False)
            for k in range(4):
                lo, hi = max(c0, L * k), min(c0 + 512, L * k + L)
                if lo >= hi:
                    continue
                for i in range(k + 1, 5):
                    w = i - k if i < 4 else 3 - k
                    piece = (R("P%d" % b, lo - c0, hi - c0), R("ID", 128 * w, 128 * w + 128), R("G", lo + L * (i - k), hi + L * (i - k)))
                    if i < 4:
                        mm(piece[0], piece[1], piece[2], False, False)
                    else:
                        fin.append((b, piece))
        tt(lv("G5", 4), R("P7", 0, 48), lv("G5", 3), A.max)
        frozen(4)
        act(R("G", 4 * L, 5 * L), IND(R(Xr, 0, W), lv("OG", 4)))
        if not last:
            ts(R("T48"), lv("F5", 4), float(V), A.is_lt, -8192.0, A.mult)
            tt(R("SHF"), R("T48"), lv("F5", 4), A.add)
            tt(R("SHG"), R("SHF"), R("U48"), A.max)
            ts(R("OAN"), R("SHG"), float(L - V), A.add)
            act(IND(R("FW%d" % r), R("OAN")), R("SL", 0, L), F.Silu)
            exchange(3 + r, "FW%d" % r, L, "LF%d" % r, 0)
        for j, (b, piece) in enumerate(fin):
            mm(piece[0], piece[1], piece[2], False, j + 1 == len(fin) or fin[j + 1][0] != b)
        for k in range(1, 5):
            tt(lv("EE", k), lv("F5", k), lv("F5", 0), A.subtract)
        ts(R("HKI"), R("G5", 48, 240), 1, A.bitwise_and)
        tt(R("NT", 0, 144), R("G5", 96, 240), R("THR", 0, 144), A.is_ge)
        ts(R("T1"), R("EE", 48, 240), -0.5, A.add)
        tt(R("T2"), R("T1"), R("NT"), A.mult)
        tt(R("C2", 220), R("NT"), R("HKI"), A.mult)
        tt(R("T3"), R("T2"), R("EE", 0, 192), A.subtract)
        ts(R("C0", 220), R("T3"), MAG * 32, A.add, MAG * 32, A.subtract)
        tt(R("C1", 220), R("T3"), R("C0", 220), A.subtract)
        if not last:
            tt(R("C3", 268), R("HKI", 0, 144), R("HKI", 48, 192), A.subtract)
            tt(R("C3", 220, 268), R("HKI", 144, 192), R("HKI", 0, 48), A.subtract)
        for j in (2, 0, 1) if last else (2, 0, 1, 3):
            dma(R("C", row=j), R("C%d" % j), "c%d" % r)
        tt(R("T1"), R("WL", 0, 192), R("CAP"), A.min)
        tt(R("T2"), R("T1"), R("BASE"), A.max)
        ts(R("OX"), R("T2"), 0.25, A.add)
        for b in range(6):
            o = R(Xr, W + 512 * b, W + 512 * b + 512)
            if b < TUNE["ev"][last]:
                ts(o, R("P%d" % b), -0.46875, A.add)
            else:
                act(o, R("P%d" % b), bias=-0.46875)
        ts(R("QB"), R("T2"), 0.0625, A.mult, -0.46875, A.add)
        ts(R("T1"), R("OX"), float(CST), A.mult)
        ts(R("T3"), R("QB"), float(1 - 16 * CST), A.mult)
        tt(R("T2"), R("T1"), R("T3"), A.add)
        cp(R("OC"), R("T2"))
        if not last:
            Xn = "X%d" % (r + 1)
            split(Xn, 0, R(Xr), "OX", V, TUNE["x"][0])
            cp(R("SD%d" % (r + 1)), IND(R(Xn, 0, V), R("OS", 0, 28)))
            exchange(r + 1, "SD%d" % (r + 1), 0, Xn, V)
            dma(R("XL", 0, 1024), R(Xn, 0, 1024), "xc%d" % r)
            dma(R("XL", 1024, 2560), R(Xn, 1024, 2560), "xc%d" % r)
            rl(R("P1", 0, 192), "ONE", Xn, 0, V)
            mm(R("P0", 0, 192), R("IDF"), R("HF"), True, False)
        else:
            nv = TUNE["x"][1]
            split("XL", 0, R(Xr), "OX", V, nv, -OFF)
            dma(X(T.y[:, 0:nv]), R("XL", 0, nv), "y")
            dma(X(T.y[:, nv:V]), R("XL", nv, V), "y")
            tt(R("T1"), R("HF"), R("GDL"), A.subtract)
            mm(R("P0", 0, 192), R("IDF"), R("T1"), True, False)
        split("ST", 16, R("C"), "OC", V, TUNE["st"][last])
        rl(R("P0", 0, 192), "FLP", "ST", 16, V, False, False)
        nv = TUNE["sp"][last]
        h1, h2 = nv - 512, V - 512
        for a, b in ((nv, h2), (0, h1), (h2, V), (h1, nv)):
            w_ = IND(R("ST"), R("OQ", a // 16, b // 16))
            if a < nv:
                cp(R("D", a, b), w_)
            else:
                act(R("D", a, b), w_)
            rl(R("P0", a // 16, b // 16), "KD", "D", a, b - a, False, b == nv)
        if not last:
            act(IND(R("F2"), R("OSP", 0, 28)), R("LF%d" % r), F.Silu)
            dma(R("FL"), R("F2", row=0))
            rl(R("P2", 0, 192), "DH", "ST", 16, V)
            ts(R("OP"), R("P0", 0, 192), 0.5, A.mult, -0.25, A.add)
            act(R("HF"), R("P0", 0, 192))
        else:
            cp(R("T3"), R("P0", 0, 192))
            for h in range(2):
                o, i_ = R("P%d" % (3 + h), 0, 128, parts=96), R("T3", 96 * h, 96 * h + 96)
                add("T", lambda o=o, i_=i_: g.tensor.transpose(o[0], i_[0], T.IDF[:]), o, (i_, R("IDF")))
                if h == 0:
                    cp(R("TT", 0, 128, parts=96), o)
                else:
                    act(R("TT", 128, 256, parts=96), o)
                for gq in range(8):
                    dma(X(T.yh[gq:gq + 1, 1536 * h:1536 * h + 1536]), R("TT", 128 * h + 16 * gq, 128 * h + 16 * gq + 16, parts=96),
                        "yh%d" % h, q="Y" if h == 0 else "S")

    hist = {}
    deps = []
    for n, op in enumerate(ops):
        d = set()
        accs = [(a, False) for a in op["r"]] + [(a, True) for a in op["w"]]
        for acc, wr in accs:
            nm, a, b, row, ps = acc
            for (m, a2, b2, row2, wr2) in hist.get(nm, []):
                if m == n or a >= b2 or a2 >= b or (row is not None and row2 is not None and row != row2):
                    continue
                o2 = ops[m]
                same = o2["e"] == op["e"] and o2["grp"] is None
                if same and op["e"] == "T":
                    continue
                if wr or wr2 or (ps and not same):
                    d.add(m)
        for acc, wr in accs:
            nm, a, b, row, ps = acc
            h = hist.setdefault(nm, [])
            if wr and row is None:
                h[:] = [x for x in h if not (a <= x[1] and x[2] <= b)]
            h.append((n, a, b, row, wr))
        deps.append(d)
    needed = set()
    for n, d in enumerate(deps):
        best = {}
        for m in d:
            if ops[m]["grp"] is None:
                best[ops[m]["e"]] = max(best.get(ops[m]["e"], -1), m)
        needed.update(best.values())
    count, val = {}, {}
    for n, op in enumerate(ops):
        if op["grp"] is None:
            if n in needed:
                count[op["e"]] = count.get(op["e"], 0) + 1
            val[n] = count.get(op["e"], 0)
    queue = {"V": g.vector, "S": g.scalar, "T": g.tensor, "G": g, "Y": g.sync}
    waited = {}
    for n, op in enumerate(ops):
        if op["fn"] is None:
            continue
        want = {}
        for m in deps[n]:
            o2 = ops[m]
            if o2["grp"] == "remote" or (o2["grp"] is not None and o2["grp"] == op["grp"]):
                continue
            if o2["grp"] is None:
                if m not in needed:
                    continue
                s, v = "s" + o2["e"], val[m]
            else:
                s, v = groups[o2["grp"]]
            want[s] = max(want.get(s, 0), v)
        for s in sorted(want):
            if waited.get((op["e"], s), 0) < want[s]:
                queue[op["e"]].wait_ge(T.sem[s], want[s])
                waited[(op["e"], s)] = want[s]
        ins = op["fn"]()
        if op["grp"] is None:
            if n in needed:
                ins.then_inc(T.sem["s" + op["e"]], 1)
        elif op["grp"] != "remote":
            ins.then_inc(T.sem[groups[op["grp"]][0]], 16)
    for e in sorted(count):
        g.wait_ge(T.sem["s" + e], count[e])
    g.wait_ge(T.sem.sent, sent[0])
    for k in sorted(groups):
        g.wait_ge(T.sem[groups[k][0]], groups[k][1])
